import numpy as np
import ml_dtypes


def mxq(x, axis, fmt="e4m3"):
    dtype, down = {"e4m3": (ml_dtypes.float8_e4m3fn, 7), "e5m2": (ml_dtypes.float8_e5m2, 14)}[fmt]
    v = np.moveaxis(np.asarray(x, np.float32).astype(ml_dtypes.bfloat16).astype(np.float64), axis, -1)
    blocks = v.reshape(v.shape[:-1] + (-1, 32))
    amax = np.abs(blocks).max(-1, keepdims=True)
    byte = np.maximum(np.where(amax > 0, np.frexp(amax)[1] - 1 + 127, 0) - down, 1)
    scale = np.exp2(byte - 127.0)
    codes = (blocks / scale).astype(np.float32).astype(dtype).astype(np.float64)
    return np.moveaxis((codes * scale).reshape(v.shape), -1, axis)


WIDE = False


def mx_kscale(k):
    if not WIDE:
        return np.ones(k)
    levels = np.array([10, -10, 5, -5, 0])
    if k % 512:
        return np.exp2(np.random.permutation(np.resize(levels, k // 32))).repeat(32)
    a = np.empty((k // 512, 16))
    for p in range(k // 512):
        a[p, :8] = np.random.permutation(np.resize(levels, 8))
        for g in range(8):
            far = levels[np.abs(levels - a[p, g]) >= 10]
            a[p, g + 8] = far[np.random.randint(len(far))]
    return np.exp2(a.ravel()).repeat(32)


def f64(x):
    return np.asarray(x).astype(np.float64)


def striped(idx):
    return np.tile(idx.reshape(-1, 16).T, (8, 1)).astype(np.uint16)


def unstriped(offs):
    return offs[:16].T.reshape(-1).astype(np.int64)


def striped8(idx):
    return np.concatenate([x.reshape(-1, 16).T for x in idx]).astype(np.uint16)


def runs(offs, k):
    lists = np.stack([offs[16 * r : 16 * r + 16].T.reshape(-1) for r in range(8)]).astype(np.int64)
    return lists[np.arange(k) % 512 // 64]


def pack_weight(w):
    k, n = w.shape
    w = f64(np.asarray(w, np.float32).astype(ml_dtypes.bfloat16)).reshape(k // 32, 32, n)
    amax = np.abs(w).max(1)
    byte = np.clip(np.where(amax > 0, np.frexp(amax)[1] - 1 + 127 - 7, 1), 1, 254)
    scaled = (w * np.exp2(127.0 - byte)[:, None, :]).reshape(k, n).astype(np.float32)
    words = np.ascontiguousarray(scaled.reshape(k // 512, 128, 4, n).transpose(0, 1, 3, 2)).astype(ml_dtypes.float8_e4m3fn).view(np.uint8)
    return words, np.ascontiguousarray(byte.astype(np.uint8).reshape(k // 512, 16, n))


def unpack_weight(words, scales):
    g, p, n, _ = words.shape
    vals = np.ascontiguousarray(words).view(ml_dtypes.float8_e4m3fn).astype(np.float64) * np.repeat(np.exp2(scales.astype(np.float64) - 127.0), 8, axis=1)[..., None]
    return vals.transpose(0, 1, 3, 2).reshape(g * 512, n)


E2M1 = np.array([0.0, 0.5, 1.0, 1.5, 2.0, 3.0, 4.0, 6.0, -0.0, -0.5, -1.0, -1.5, -2.0, -3.0, -4.0, -6.0])


def pack_fp4(w):
    k, n = w.shape
    w = f64(np.asarray(w, np.float32).astype(ml_dtypes.bfloat16)).reshape(k // 32, 32, n)
    amax = np.abs(w).max(1)
    mant, ex = np.frexp(amax / 6.0)
    byte = np.clip(np.where(amax > 0, np.where(mant > 0.5, ex, ex - 1) + 127, 1), 1, 254)
    scaled = (w * np.exp2(127.0 - byte)[:, None, :]).reshape(k, n).astype(np.float32)
    c = np.ascontiguousarray(scaled.reshape(k // 512, 128, 4, n).transpose(0, 1, 3, 2)).astype(ml_dtypes.float4_e2m1fn).view(np.uint8) & 0xF
    words = (c[..., 0::2] | (c[..., 1::2] << 4)).reshape(k // 512, 128, 2 * n)
    return np.ascontiguousarray(words), np.ascontiguousarray(byte.astype(np.uint8).reshape(k // 512, 16, n))


def unpack_fp4(words, scales):
    g, _, n = scales.shape
    words = np.ascontiguousarray(words).reshape(g, 128, n, 2)
    nib = np.empty((g, 128, n, 4), np.uint8)
    nib[..., 0::2] = words & 0xF
    nib[..., 1::2] = words >> 4
    vals = E2M1[nib] * np.repeat(np.exp2(scales.astype(np.float64) - 127.0), 8, axis=1)[..., None]
    return vals.transpose(0, 1, 3, 2).reshape(g * 512, n)


def planes(y):
    n, m = y.shape
    v = y.astype(np.float32).astype(ml_dtypes.bfloat16).astype(np.float64).reshape(n // 32, 32, m)
    top = np.abs(v).max(1)
    byte = np.clip(np.where(top > 0, np.frexp(top)[1] - 1 + 127 - 7, 1), 1, 254)
    codes = (v * np.exp2(127.0 - byte)[:, None, :]).reshape(n, m).astype(np.float32).astype(ml_dtypes.float8_e4m3fn).view(np.uint8)
    words = codes.reshape(n // 512, 128, 4, m).transpose(0, 1, 3, 2)
    return np.ascontiguousarray(words), np.ascontiguousarray(byte.astype(np.uint8).reshape(n // 512, 16, m))


K, T, S, N, U, H = 512, 2048, 512, 512, 1024, 512


def setup_inputs():
    n = np.random.standard_normal
    s = mx_kscale(K)[:, None]
    u = mx_kscale(H)
    packed_xT = pack_weight(n((K, T)) * s)
    packed_w2 = pack_fp4(n((H, N)) / np.sqrt(H) / u[:, None])
    return {
        "x_words": packed_xT[0],
        "x_scales": packed_xT[1],
        "w1": (n((K, H)) / np.sqrt(K) / s * u).astype(np.float32),
        "mem": (n((H, U)) * u[:, None]).astype(np.float32),
        "w2_words": packed_w2[0],
        "w2_scales": packed_w2[1],
        "offs": striped(np.random.permutation(T)[:S]),
        "slot": striped8(np.stack([np.random.permutation(U)[:S] for _ in range(8)])),
    }


def reference(x_words, x_scales, w1, mem, w2_words, w2_scales, offs, slot):
    xq = unpack_weight(x_words, x_scales)[:, unstriped(offs)]
    y = mxq(f64(w1), 0, "e4m3").T @ xq
    nw = np.maximum(y, 0.75 * (f64(mem)[np.arange(H)[:, None], runs(slot, H)]))
    dm = 0.75 * f64(mem)
    z = dm.copy()
    z[np.arange(H)[:, None], runs(slot, H)] = nw
    out_0 = unpack_fp4(w2_words, w2_scales).T @ mxq(z, 0, "e4m3")
    return (out_0,) + planes(out_0)

@@ -1,0 +1,207 @@
+from contextlib import ExitStack
+
+import concourse.mybir as mybir
+
+F32 = mybir.dt.float32
+BF16 = mybir.dt.bfloat16
+I32 = mybir.dt.int32
+U32 = mybir.dt.uint32
+U16 = mybir.dt.uint16
+U8 = mybir.dt.uint8
+FP8X4 = mybir.dt.float8_e4m3fn_x4
+FP4X4 = mybir.dt.float4_e2m1fn_x4
+COPY = mybir.ActivationFunctionType.Copy
+MULT = mybir.AluOpType.mult
+MAX = mybir.AluOpType.max
+
+K, T, S, H, U, N = 512, 2048, 512, 512, 1024, 512
+P = 128
+PACK = 4
+BANK = 512
+DECAY = 0.75
+FLOPS = 2 * K * H * S + 2 * H * N * U
+TILE_ORDER = (2, 0, 1, 3)
+CHUNKS = (128, 128, 256, 256, 128, 128)
+CODE_STORES = (2, 4, 5)
+SCALAR_ROUNDS = (2, 3)
+
+
+def load_scale_rows(queue, plane, rows):
+    for q in range(4):
+        queue.dma_start(out=plane[32 * q : 32 * q + 4, :].bitcast(I32), in_=rows[4 * q : 4 * q + 4, :].bitcast(I32))
+
+
+def tile_picked_decaypage_none_po_kernel(tc, x_words, x_scales, w1, mem, w2_words, w2_scales, offs, slot, out_0, out_1, out_2):
+    nc = tc.nc
+    with ExitStack() as ctx:
+        keep = ctx.enter_context(tc.tile_pool(name="keep", bufs=1))
+        ring = ctx.enter_context(tc.tile_pool(name="ring", bufs=2))
+        psum = ctx.enter_context(tc.psum_pool(name="psum", bufs=1))
+
+        offs_sb = keep.tile([P, S // 16], U16)
+        slot_sb = keep.tile([P, S // 16], U16)
+        w1_raw = keep.tile([P, PACK, H], F32)
+        x_table = keep.tile([P, T], U32)
+        xs_table = keep.tile([P, T], U8)
+        w2_raw = keep.tile([P, 2 * N], U8)
+        w2s_raw = keep.tile([P, N], U8)
+        mem_sb = {}
+        mem_rows = mem.rearrange("(p t) w -> t p w", t=PACK)
+
+        nc.vector.memset(xs_table[:].bitcast(I32), 0)
+        nc.vector.memset(w2s_raw[:].bitcast(I32), 0)
+
+        def load_mem(t):
+            mem_sb[t] = ring.tile([P, U], F32, name="mem_sb")
+            nc.sync.dma_start(out=mem_sb[t][:], in_=mem_rows[t])
+
+        nc.sync.dma_start(out=offs_sb[:], in_=offs)
+        nc.scalar.dma_start(out=w2_raw[:].bitcast(I32), in_=w2_words[0].bitcast(I32))
+        nc.sync.dma_start(out=slot_sb[:], in_=slot)
+        nc.sync.dma_start(out=w1_raw[:], in_=w1.rearrange("(p j) c -> p j c", j=PACK))
+        load_mem(TILE_ORDER[0])
+        nc.sync.dma_start(out=x_table[:].bitcast(I32), in_=x_words[0].rearrange("p n t -> p (n t)").bitcast(I32))
+        load_mem(TILE_ORDER[1])
+        load_scale_rows(nc.scalar, xs_table, x_scales[0])
+        load_scale_rows(nc.sync, w2s_raw, w2_scales[0])
+
+        w2_dealt = keep.tile([P, 2 * N], U8, align_bytes=64)
+        w2s_dealt = keep.tile([P, N], U8, align_bytes=64)
+        nc.vector.tensor_copy(
+            out=w2_dealt[:].rearrange("p (t m b) -> p t m b", t=PACK, b=2),
+            in_=w2_raw[:].rearrange("p (m t b) -> p t m b", t=PACK, b=2),
+        )
+
+        xs_picked = keep.tile([P, S], U8, align_bytes=64)
+        nc.vector.tensor_copy(out=xs_picked[:], in_=xs_table[:].indirect(offs_sb[:]))
+
+        w1_bf = keep.tile([P, PACK * H], BF16, align_bytes=64)
+        nc.scalar.copy(
+            out=w1_bf[:].rearrange("p (t m j) -> p m t j", t=PACK, j=PACK),
+            in_=w1_raw[:].rearrange("p j (m t) -> p m t j", t=PACK),
+        )
+
+        old = [keep.tile([P, S], F32, name=f"old{t}") for t in range(PACK)]
+
+        def fetch_old(t):
+            nc.vector.tensor_copy(out=old[t][:], in_=mem_sb[t][:].indirect(slot_sb[:]))
+
+        fetch_old(TILE_ORDER[0])
+
+        w1_codes = keep.tile([P, H], U32, align_bytes=64)
+        w1_scales = keep.tile([P, H], U8, align_bytes=64)
+        nc.vector.quantize_mx(out=w1_codes[:].bitcast(FP8X4), scales=w1_scales[:], in_=w1_bf[:])
+
+        x_picked = keep.tile([P, S], U32, align_bytes=64)
+        nc.vector.tensor_copy(out=x_picked[:], in_=x_table[:].indirect(offs_sb[:]))
+
+        z_bf = keep.tile([P, U, PACK], BF16, align_bytes=64)
+        z_last = None
+        for i, t in enumerate(TILE_ORDER):
+            y = psum.tile([P, S], F32, name="y", bufs=2)
+            cols = slice(t * P, (t + 1) * P)
+            nc.tensor.matmul_mx(
+                out=y[:],
+                lhsT=w1_codes[:, cols].bitcast(FP8X4),
+                lhsT_scale=w1_scales[:, cols],
+                rhs=x_picked[:].bitcast(FP8X4),
+                rhs_scale=xs_picked[:],
+                start=True,
+                stop=True,
+            )
+            z = ring.tile([P, U], F32, name="z", bufs=3)
+            nc.scalar.activation(out=z[:], in_=mem_sb[t][:], func=COPY, scale=DECAY)
+            if i + 2 < PACK:
+                load_mem(TILE_ORDER[i + 2])
+            if i == 0:
+                fetch_old(TILE_ORDER[1])
+            new = ring.tile([P, S], F32, name="new")
+            nc.vector.scalar_tensor_tensor(out=new[:], in0=old[t][:], scalar=DECAY, in1=y[:], op0=MULT, op1=MAX)
+            if 0 < i < PACK - 1:
+                fetch_old(TILE_ORDER[i + 1])
+            if i == PACK - 1:
+                nc.vector.tensor_copy(
+                    out=w2s_dealt[:].rearrange("p (t m) -> p t m", t=PACK),
+                    in_=w2s_raw[:].rearrange("p (m t) -> p t m", t=PACK),
+                )
+            nc.vector.tensor_copy(out=z[:].indirect(slot_sb[:]), in_=new[:])
+            if i + 1 < PACK:
+                nc.scalar.copy(out=z_bf[:, :, t], in_=z[:])
+            else:
+                z_last = z
+
+        z_codes = keep.tile([P, U], U32, align_bytes=64)
+        z_scales = keep.tile([P, U], U8, align_bytes=64)
+        o_codes = keep.tile([P, U], U32, align_bytes=64)
+        o_scales = keep.tile([P, U], U8, align_bytes=64)
+        out_rows = out_0.rearrange("(p t) w -> p t w", t=PACK)
+        code_rows = out_1[0].rearrange("p n t -> p (n t)").bitcast(I32)
+        starts = [sum(CHUNKS[:c]) for c in range(len(CHUNKS) + 1)]
+        spans = [slice(starts[c], starts[c + 1]) for c in range(len(CHUNKS))]
+        last_t = TILE_ORDER[-1]
+        results = {}
+        rounded = {}
+
+        def round_last(c):
+            if c in SCALAR_ROUNDS:
+                nc.scalar.copy(out=z_bf[:, spans[c], last_t], in_=z_last[:, spans[c]])
+            else:
+                nc.vector.tensor_copy(out=z_bf[:, spans[c], last_t], in_=z_last[:, spans[c]])
+
+        def second_product(c):
+            width = CHUNKS[c]
+            nc.vector.quantize_mx(
+                out=z_codes[:, spans[c]].bitcast(FP8X4),
+                scales=z_scales[:, spans[c]],
+                in_=z_bf[:, spans[c], :].rearrange("p w t -> p (w t)"),
+            )
+            res = keep.tile([P, PACK, width], F32, name=f"res{c}")
+            per_bank = BANK // width
+            for t0 in range(0, PACK, per_bank):
+                acc = psum.tile([P, per_bank, width], F32, name="acc", bufs=6)
+                for j in range(per_bank):
+                    t = t0 + j
+                    nc.tensor.matmul_mx(
+                        out=acc[:, j, :],
+                        lhsT=w2_dealt[:, 2 * P * t : 2 * P * (t + 1)].bitcast(FP4X4),
+                        lhsT_scale=w2s_dealt[:, P * t : P * (t + 1)],
+                        rhs=z_codes[:, spans[c]].bitcast(FP8X4),
+                        rhs_scale=z_scales[:, spans[c]],
+                        start=True,
+                        stop=True,
+                    )
+                nc.scalar.copy(out=res[:, t0 : t0 + per_bank, :], in_=acc[:])
+            nc.sync.dma_start(out=out_rows[:, :, spans[c]], in_=res[:])
+            results[c] = res
+
+        def round_result(c):
+            o_bf = keep.tile([P, CHUNKS[c], PACK], BF16, name=f"o_bf{c}", align_bytes=64)
+            nc.vector.tensor_copy(out=o_bf[:], in_=results[c][:].rearrange("p t w -> p w t"))
+            rounded[c] = o_bf
+
+        def quantize_result(c):
+            nc.vector.quantize_mx(
+                out=o_codes[:, spans[c]].bitcast(FP8X4),
+                scales=o_scales[:, spans[c]],
+                in_=rounded[c][:].rearrange("p w t -> p (w t)"),
+            )
+            if c in CODE_STORES:
+                before = [e for e in CODE_STORES if e < c]
+                first = starts[before[-1] + 1] if before else 0
+                nc.sync.dma_start(out=code_rows[:, first : starts[c + 1]], in_=o_codes[:, first : starts[c + 1]].bitcast(I32))
+
+        n_chunks = len(CHUNKS)
+        for c in range(4):
+            round_last(c)
+        for c in range(n_chunks):
+            second_product(c)
+            if c + 4 < n_chunks:
+                round_last(c + 4)
+        round_result(0)
+        for c in range(n_chunks):
+            if c + 1 < n_chunks:
+                round_result(c + 1)
+            quantize_result(c)
+        for q in range(4):
+            queue = nc.sync if q % 2 == 0 else nc.scalar
+            queue.dma_start(out=out_2[0, 4 * q : 4 * q + 4, :].bitcast(I32), in_=o_scales[32 * q : 32 * q + 4, :].bitcast(I32))

@@ -17,13 +17,18 @@ MAX = mybir.AluOpType.max
 K, T, S, H, U, N = 512, 2048, 512, 512, 1024, 512
 P = 128
 PACK = 4
-BANK = 512
 DECAY = 0.75
 FLOPS = 2 * K * H * S + 2 * H * N * U
 TILE_ORDER = (2, 0, 1, 3)
-CHUNKS = (128, 128, 256, 256, 128, 128)
-CODE_STORES = (2, 4, 5)
-SCALAR_ROUNDS = (2, 3)
+W1_VECTOR = 32
+CHUNK = 128
+N_CHUNKS = U // CHUNK
+VECTOR_ROUNDS = ((0, 1), (1, 2), (2, 3))
+SCALAR_ROUNDS = ((3, 5), (5, 8))
+Z_QUANT = ((0, 1), (1, 2), (2, 3), (3, 5), (5, 7), (7, 8))
+RESULT_STORES = ((0, 1), (1, 2), (2, 4), (4, 6), (6, 8))
+OUT_QUANT = ((0, 1), (1, 2), (2, 4), (4, 6), (6, 7), (7, 8))
+CODE_STORES = ((0, 4), (4, 7), (7, 8))
 
 
 def load_scale_rows(queue, plane, rows):
@@ -31,11 +36,19 @@ def load_scale_rows(queue, plane, rows):
         queue.dma_start(out=plane[32 * q : 32 * q + 4, :].bitcast(I32), in_=rows[4 * q : 4 * q + 4, :].bitcast(I32))
 
 
+def columns(run):
+    return slice(run[0] * CHUNK, run[1] * CHUNK)
+
+
+def ending_at(runs, c):
+    return [run for run in runs if run[1] == c + 1]
+
+
 def tile_picked_decaypage_none_po_kernel(tc, x_words, x_scales, w1, mem, w2_words, w2_scales, offs, slot, out_0, out_1, out_2):
     nc = tc.nc
     with ExitStack() as ctx:
         keep = ctx.enter_context(tc.tile_pool(name="keep", bufs=1))
-        ring = ctx.enter_context(tc.tile_pool(name="ring", bufs=2))
+        ring = ctx.enter_context(tc.tile_pool(name="ring", bufs=3))
         psum = ctx.enter_context(tc.psum_pool(name="psum", bufs=1))
 
         offs_sb = keep.tile([P, S // 16], U16)
@@ -45,24 +58,21 @@ def tile_picked_decaypage_none_po_kernel(tc, x_words, x_scales, w1, mem, w2_word
         xs_table = keep.tile([P, T], U8)
         w2_raw = keep.tile([P, 2 * N], U8)
         w2s_raw = keep.tile([P, N], U8)
-        mem_sb = {}
+        mem_sb = [keep.tile([P, U], F32, name=f"mem{t}") for t in range(PACK)]
         mem_rows = mem.rearrange("(p t) w -> t p w", t=PACK)
 
         nc.vector.memset(xs_table[:].bitcast(I32), 0)
         nc.vector.memset(w2s_raw[:].bitcast(I32), 0)
 
-        def load_mem(t):
-            mem_sb[t] = ring.tile([P, U], F32, name="mem_sb")
-            nc.sync.dma_start(out=mem_sb[t][:], in_=mem_rows[t])
-
         nc.sync.dma_start(out=offs_sb[:], in_=offs)
         nc.scalar.dma_start(out=w2_raw[:].bitcast(I32), in_=w2_words[0].bitcast(I32))
         nc.sync.dma_start(out=slot_sb[:], in_=slot)
         nc.sync.dma_start(out=w1_raw[:], in_=w1.rearrange("(p j) c -> p j c", j=PACK))
-        load_mem(TILE_ORDER[0])
+        load_scale_rows(nc.sync, xs_table, x_scales[0])
+        nc.sync.dma_start(out=mem_sb[TILE_ORDER[0]][:], in_=mem_rows[TILE_ORDER[0]])
         nc.sync.dma_start(out=x_table[:].bitcast(I32), in_=x_words[0].rearrange("p n t -> p (n t)").bitcast(I32))
-        load_mem(TILE_ORDER[1])
-        load_scale_rows(nc.scalar, xs_table, x_scales[0])
+        for t in TILE_ORDER[1:]:
+            nc.sync.dma_start(out=mem_sb[t][:], in_=mem_rows[t])
         load_scale_rows(nc.sync, w2s_raw, w2_scales[0])
 
         w2_dealt = keep.tile([P, 2 * N], U8, align_bytes=64)
@@ -72,14 +82,14 @@ def tile_picked_decaypage_none_po_kernel(tc, x_words, x_scales, w1, mem, w2_word
             in_=w2_raw[:].rearrange("p (m t b) -> p t m b", t=PACK, b=2),
         )
 
+        w1_bf = keep.tile([P, PACK * H], BF16, align_bytes=64)
+        w1_dst = w1_bf[:].rearrange("p (t m j) -> p m j t", t=PACK, j=PACK)
+        w1_src = w1_raw[:].rearrange("p j (m t) -> p m j t", t=PACK)
+        nc.vector.tensor_copy(out=w1_dst[:, :W1_VECTOR], in_=w1_src[:, :W1_VECTOR])
+        nc.scalar.copy(out=w1_dst[:, W1_VECTOR:], in_=w1_src[:, W1_VECTOR:])
+
         xs_picked = keep.tile([P, S], U8, align_bytes=64)
         nc.vector.tensor_copy(out=xs_picked[:], in_=xs_table[:].indirect(offs_sb[:]))
-
-        w1_bf = keep.tile([P, PACK * H], BF16, align_bytes=64)
-        nc.scalar.copy(
-            out=w1_bf[:].rearrange("p (t m j) -> p m t j", t=PACK, j=PACK),
-            in_=w1_raw[:].rearrange("p j (m t) -> p m t j", t=PACK),
-        )
 
         old = [keep.tile([P, S], F32, name=f"old{t}") for t in range(PACK)]
 
@@ -94,10 +104,17 @@ def tile_picked_decaypage_none_po_kernel(tc, x_words, x_scales, w1, mem, w2_word
 
         x_picked = keep.tile([P, S], U32, align_bytes=64)
         nc.vector.tensor_copy(out=x_picked[:], in_=x_table[:].indirect(offs_sb[:]))
+        fetch_old(TILE_ORDER[1])
 
         z_bf = keep.tile([P, U, PACK], BF16, align_bytes=64)
-        z_last = None
-        for i, t in enumerate(TILE_ORDER):
+        page = {}
+        new = {}
+
+        def decay(t):
+            page[t] = ring.tile([P, U], F32, name="page")
+            nc.scalar.activation(out=page[t][:], in_=mem_sb[t][:], func=COPY, scale=DECAY)
+
+        def raise_old(t):
             y = psum.tile([P, S], F32, name="y", bufs=2)
             cols = slice(t * P, (t + 1) * P)
             nc.tensor.matmul_mx(
@@ -109,99 +126,88 @@ def tile_picked_decaypage_none_po_kernel(tc, x_words, x_scales, w1, mem, w2_word
                 start=True,
                 stop=True,
             )
-            z = ring.tile([P, U], F32, name="z", bufs=3)
-            nc.scalar.activation(out=z[:], in_=mem_sb[t][:], func=COPY, scale=DECAY)
+            new[t] = ring.tile([P, S], F32, name="new")
+            nc.vector.scalar_tensor_tensor(out=new[t][:], in0=old[t][:], scalar=DECAY, in1=y[:], op0=MULT, op1=MAX)
+
+        for t in TILE_ORDER[:3]:
+            decay(t)
+        raise_old(TILE_ORDER[0])
+        for i, t in enumerate(TILE_ORDER):
+            if i + 1 < PACK:
+                raise_old(TILE_ORDER[i + 1])
             if i + 2 < PACK:
-                load_mem(TILE_ORDER[i + 2])
-            if i == 0:
-                fetch_old(TILE_ORDER[1])
-            new = ring.tile([P, S], F32, name="new")
-            nc.vector.scalar_tensor_tensor(out=new[:], in0=old[t][:], scalar=DECAY, in1=y[:], op0=MULT, op1=MAX)
-            if 0 < i < PACK - 1:
-                fetch_old(TILE_ORDER[i + 1])
+                fetch_old(TILE_ORDER[i + 2])
             if i == PACK - 1:
                 nc.vector.tensor_copy(
                     out=w2s_dealt[:].rearrange("p (t m) -> p t m", t=PACK),
                     in_=w2s_raw[:].rearrange("p (m t) -> p t m", t=PACK),
                 )
-            nc.vector.tensor_copy(out=z[:].indirect(slot_sb[:]), in_=new[:])
+            nc.vector.tensor_copy(out=page[t][:].indirect(slot_sb[:]), in_=new[t][:])
             if i + 1 < PACK:
-                nc.scalar.copy(out=z_bf[:, :, t], in_=z[:])
-            else:
-                z_last = z
+                nc.scalar.copy(out=z_bf[:, :, t], in_=page[t][:])
+            if i == 0:
+                decay(TILE_ORDER[3])
+        last_t = TILE_ORDER[-1]
 
         z_codes = keep.tile([P, U], U32, align_bytes=64)
         z_scales = keep.tile([P, U], U8, align_bytes=64)
+        res = keep.tile([P, PACK, U], F32)
+        o_bf = keep.tile([P, U, PACK], BF16, align_bytes=64)
         o_codes = keep.tile([P, U], U32, align_bytes=64)
         o_scales = keep.tile([P, U], U8, align_bytes=64)
         out_rows = out_0.rearrange("(p t) w -> p t w", t=PACK)
         code_rows = out_1[0].rearrange("p n t -> p (n t)").bitcast(I32)
-        starts = [sum(CHUNKS[:c]) for c in range(len(CHUNKS) + 1)]
-        spans = [slice(starts[c], starts[c + 1]) for c in range(len(CHUNKS))]
-        last_t = TILE_ORDER[-1]
-        results = {}
-        rounded = {}
 
-        def round_last(c):
-            if c in SCALAR_ROUNDS:
-                nc.scalar.copy(out=z_bf[:, spans[c], last_t], in_=z_last[:, spans[c]])
-            else:
-                nc.vector.tensor_copy(out=z_bf[:, spans[c], last_t], in_=z_last[:, spans[c]])
+        def quantize(codes, scales, values, cols):
+            nc.vector.quantize_mx(
+                out=codes[:, cols].bitcast(FP8X4),
+                scales=scales[:, cols],
+                in_=values[:, cols, :].rearrange("p w t -> p (w t)"),
+            )
 
         def second_product(c):
-            width = CHUNKS[c]
-            nc.vector.quantize_mx(
-                out=z_codes[:, spans[c]].bitcast(FP8X4),
-                scales=z_scales[:, spans[c]],
-                in_=z_bf[:, spans[c], :].rearrange("p w t -> p (w t)"),
-            )
-            res = keep.tile([P, PACK, width], F32, name=f"res{c}")
-            per_bank = BANK // width
-            for t0 in range(0, PACK, per_bank):
-                acc = psum.tile([P, per_bank, width], F32, name="acc", bufs=6)
-                for j in range(per_bank):
-                    t = t0 + j
-                    nc.tensor.matmul_mx(
-                        out=acc[:, j, :],
-                        lhsT=w2_dealt[:, 2 * P * t : 2 * P * (t + 1)].bitcast(FP4X4),
-                        lhsT_scale=w2s_dealt[:, P * t : P * (t + 1)],
-                        rhs=z_codes[:, spans[c]].bitcast(FP8X4),
-                        rhs_scale=z_scales[:, spans[c]],
-                        start=True,
-                        stop=True,
-                    )
-                nc.scalar.copy(out=res[:, t0 : t0 + per_bank, :], in_=acc[:])
-            nc.sync.dma_start(out=out_rows[:, :, spans[c]], in_=res[:])
-            results[c] = res
+            cols = columns((c, c + 1))
+            acc = psum.tile([P, PACK, CHUNK], F32, name="acc", bufs=6)
+            for t in range(PACK):
+                nc.tensor.matmul_mx(
+                    out=acc[:, t, :],
+                    lhsT=w2_dealt[:, 2 * P * t : 2 * P * (t + 1)].bitcast(FP4X4),
+                    lhsT_scale=w2s_dealt[:, P * t : P * (t + 1)],
+                    rhs=z_codes[:, cols].bitcast(FP8X4),
+                    rhs_scale=z_scales[:, cols],
+                    start=True,
+                    stop=True,
+                )
+            nc.scalar.copy(out=res[:, :, cols], in_=acc[:])
+            for run in ending_at(RESULT_STORES, c):
+                nc.sync.dma_start(out=out_rows[:, :, columns(run)], in_=res[:, :, columns(run)])
 
-        def round_result(c):
-            o_bf = keep.tile([P, CHUNKS[c], PACK], BF16, name=f"o_bf{c}", align_bytes=64)
-            nc.vector.tensor_copy(out=o_bf[:], in_=results[c][:].rearrange("p t w -> p w t"))
-            rounded[c] = o_bf
+        for run in SCALAR_ROUNDS:
+            nc.scalar.copy(out=z_bf[:, columns(run), last_t], in_=page[last_t][:, columns(run)])
+        nc.vector.tensor_copy(out=z_bf[:, columns(VECTOR_ROUNDS[0]), last_t], in_=page[last_t][:, columns(VECTOR_ROUNDS[0])])
+        for i, run in enumerate(Z_QUANT):
+            if i + 1 < len(VECTOR_ROUNDS):
+                ahead = columns(VECTOR_ROUNDS[i + 1])
+                nc.vector.tensor_copy(out=z_bf[:, ahead, last_t], in_=page[last_t][:, ahead])
+            quantize(z_codes, z_scales, z_bf, columns(run))
+            for c in range(run[0], run[1]):
+                second_product(c)
 
-        def quantize_result(c):
-            nc.vector.quantize_mx(
-                out=o_codes[:, spans[c]].bitcast(FP8X4),
-                scales=o_scales[:, spans[c]],
-                in_=rounded[c][:].rearrange("p w t -> p (w t)"),
-            )
-            if c in CODE_STORES:
-                before = [e for e in CODE_STORES if e < c]
-                first = starts[before[-1] + 1] if before else 0
-                nc.sync.dma_start(out=code_rows[:, first : starts[c + 1]], in_=o_codes[:, first : starts[c + 1]].bitcast(I32))
+        def round_result(run):
+            dst = o_bf[:, columns(run), :].rearrange("p (c i) t -> p c t i", i=4)
+            src = res[:, :, columns(run)].rearrange("p t (c i) -> p c t i", i=4)
+            if run[1] == N_CHUNKS:
+                nc.scalar.copy(out=dst, in_=src)
+            else:
+                nc.vector.tensor_copy(out=dst, in_=src)
 
-        n_chunks = len(CHUNKS)
-        for c in range(4):
-            round_last(c)
-        for c in range(n_chunks):
-            second_product(c)
-            if c + 4 < n_chunks:
-                round_last(c + 4)
-        round_result(0)
-        for c in range(n_chunks):
-            if c + 1 < n_chunks:
-                round_result(c + 1)
-            quantize_result(c)
+        round_result(OUT_QUANT[0])
+        for i, run in enumerate(OUT_QUANT):
+            if i + 1 < len(OUT_QUANT):
+                round_result(OUT_QUANT[i + 1])
+            quantize(o_codes, o_scales, o_bf, columns(run))
+            for stored in ending_at(CODE_STORES, run[1] - 1):
+                nc.sync.dma_start(out=code_rows[:, columns(stored)], in_=o_codes[:, columns(stored)].bitcast(I32))
         for q in range(4):
             queue = nc.sync if q % 2 == 0 else nc.scalar
             queue.dma_start(out=out_2[0, 4 * q : 4 * q + 4, :].bitcast(I32), in_=o_scales[32 * q : 32 * q + 4, :].bitcast(I32))

@@ -26,7 +26,7 @@ N_CHUNKS = U // CHUNK
 VECTOR_ROUNDS = ((0, 1), (1, 2), (2, 3))
 SCALAR_ROUNDS = ((3, 5), (5, 8))
 Z_QUANT = ((0, 1), (1, 2), (2, 3), (3, 5), (5, 7), (7, 8))
-RESULT_STORES = ((0, 1), (1, 2), (2, 4), (4, 6), (6, 8))
+RESULT_STORES = ((1, 2), (2, 4), (4, 6), (6, 8))
 OUT_QUANT = ((0, 1), (1, 2), (2, 4), (4, 6), (6, 7), (7, 8))
 CODE_STORES = ((0, 4), (4, 7), (7, 8))
 
@@ -154,31 +154,35 @@ def tile_picked_decaypage_none_po_kernel(tc, x_words, x_scales, w1, mem, w2_word
         res = keep.tile([P, PACK, U], F32)
         o_bf = keep.tile([P, U, PACK], BF16, align_bytes=64)
         o_codes = keep.tile([P, U], U32, align_bytes=64)
-        o_scales = keep.tile([P, U], U8, align_bytes=64)
+        o_scales = keep.tile([P, U // 4], U8, align_bytes=64)
         out_rows = out_0.rearrange("(p t) w -> p t w", t=PACK)
         code_rows = out_1[0].rearrange("p n t -> p (n t)").bitcast(I32)
 
         def quantize(codes, scales, values, cols):
             nc.vector.quantize_mx(
                 out=codes[:, cols].bitcast(FP8X4),
-                scales=scales[:, cols],
+                scales=scales,
                 in_=values[:, cols, :].rearrange("p w t -> p (w t)"),
             )
 
         def second_product(c):
             cols = columns((c, c + 1))
-            acc = psum.tile([P, PACK, CHUNK], F32, name="acc", bufs=6)
-            for t in range(PACK):
-                nc.tensor.matmul_mx(
-                    out=acc[:, t, :],
-                    lhsT=w2_dealt[:, 2 * P * t : 2 * P * (t + 1)].bitcast(FP4X4),
-                    lhsT_scale=w2s_dealt[:, P * t : P * (t + 1)],
-                    rhs=z_codes[:, cols].bitcast(FP8X4),
-                    rhs_scale=z_scales[:, cols],
-                    start=True,
-                    stop=True,
-                )
-            nc.scalar.copy(out=res[:, :, cols], in_=acc[:])
+            group = 2 if c == 0 else PACK
+            for t0 in range(0, PACK, group):
+                acc = psum.tile([P, group, CHUNK], F32, name="acc", bufs=6)
+                for t in range(t0, t0 + group):
+                    nc.tensor.matmul_mx(
+                        out=acc[:, t - t0, :],
+                        lhsT=w2_dealt[:, 2 * P * t : 2 * P * (t + 1)].bitcast(FP4X4),
+                        lhsT_scale=w2s_dealt[:, P * t : P * (t + 1)],
+                        rhs=z_codes[:, cols].bitcast(FP8X4),
+                        rhs_scale=z_scales[:, cols],
+                        start=True,
+                        stop=True,
+                    )
+                nc.scalar.copy(out=res[:, t0 : t0 + group, cols], in_=acc[:])
+                if c == 0:
+                    nc.sync.dma_start(out=out_rows[:, t0 : t0 + group, cols], in_=res[:, t0 : t0 + group, cols])
             for run in ending_at(RESULT_STORES, c):
                 nc.sync.dma_start(out=out_rows[:, :, columns(run)], in_=res[:, :, columns(run)])
 
@@ -189,7 +193,7 @@ def tile_picked_decaypage_none_po_kernel(tc, x_words, x_scales, w1, mem, w2_word
             if i + 1 < len(VECTOR_ROUNDS):
                 ahead = columns(VECTOR_ROUNDS[i + 1])
                 nc.vector.tensor_copy(out=z_bf[:, ahead, last_t], in_=page[last_t][:, ahead])
-            quantize(z_codes, z_scales, z_bf, columns(run))
+            quantize(z_codes, z_scales[:, columns(run)], z_bf, columns(run))
             for c in range(run[0], run[1]):
                 second_product(c)
 
@@ -205,9 +209,11 @@ def tile_picked_decaypage_none_po_kernel(tc, x_words, x_scales, w1, mem, w2_word
         for i, run in enumerate(OUT_QUANT):
             if i + 1 < len(OUT_QUANT):
                 round_result(OUT_QUANT[i + 1])
-            quantize(o_codes, o_scales, o_bf, columns(run))
+            quarter = run[0] // 2
+            local = columns((run[0] - 2 * quarter, run[1] - 2 * quarter))
+            quantize(o_codes, o_scales[4 * quarter :, local], o_bf, columns(run))
             for stored in ending_at(CODE_STORES, run[1] - 1):
                 nc.sync.dma_start(out=code_rows[:, columns(stored)], in_=o_codes[:, columns(stored)].bitcast(I32))
         for q in range(4):
             queue = nc.sync if q % 2 == 0 else nc.scalar
-            queue.dma_start(out=out_2[0, 4 * q : 4 * q + 4, :].bitcast(I32), in_=o_scales[32 * q : 32 * q + 4, :].bitcast(I32))
+            queue.dma_start(out=out_2[0, 4 * q : 4 * q + 4, :].bitcast(I32).rearrange("r (j c) -> j r c", j=4), in_=o_scales[32 * q : 32 * q + 16, :].bitcast(I32))

@@ -65,7 +65,6 @@ def tile_picked_decaypage_none_po_kernel(tc, x_words, x_scales, w1, mem, w2_word
         nc.vector.memset(w2s_raw[:].bitcast(I32), 0)
 
         nc.sync.dma_start(out=offs_sb[:], in_=offs)
-        nc.scalar.dma_start(out=w2_raw[:].bitcast(I32), in_=w2_words[0].bitcast(I32))
         nc.sync.dma_start(out=slot_sb[:], in_=slot)
         nc.sync.dma_start(out=w1_raw[:], in_=w1.rearrange("(p j) c -> p j c", j=PACK))
         load_scale_rows(nc.sync, xs_table, x_scales[0])
@@ -73,11 +72,12 @@ def tile_picked_decaypage_none_po_kernel(tc, x_words, x_scales, w1, mem, w2_word
         nc.sync.dma_start(out=x_table[:].bitcast(I32), in_=x_words[0].rearrange("p n t -> p (n t)").bitcast(I32))
         for t in TILE_ORDER[1:]:
             nc.sync.dma_start(out=mem_sb[t][:], in_=mem_rows[t])
+        nc.sync.dma_start(out=w2_raw[:].bitcast(I32), in_=w2_words[0].bitcast(I32))
         load_scale_rows(nc.sync, w2s_raw, w2_scales[0])
 
         w2_dealt = keep.tile([P, 2 * N], U8, align_bytes=64)
         w2s_dealt = keep.tile([P, N], U8, align_bytes=64)
-        nc.vector.tensor_copy(
+        nc.gpsimd.tensor_copy(
             out=w2_dealt[:].rearrange("p (t m b) -> p t m b", t=PACK, b=2),
             in_=w2_raw[:].rearrange("p (m t b) -> p t m b", t=PACK, b=2),
         )
@@ -138,7 +138,7 @@ def tile_picked_decaypage_none_po_kernel(tc, x_words, x_scales, w1, mem, w2_word
             if i + 2 < PACK:
                 fetch_old(TILE_ORDER[i + 2])
             if i == PACK - 1:
-                nc.vector.tensor_copy(
+                nc.gpsimd.tensor_copy(
                     out=w2s_dealt[:].rearrange("p (t m) -> p t m", t=PACK),
                     in_=w2s_raw[:].rearrange("p (m t) -> p t m", t=PACK),
                 )

from contextlib import ExitStack

import concourse.mybir as mybir

F32 = mybir.dt.float32
BF16 = mybir.dt.bfloat16
I32 = mybir.dt.int32
U32 = mybir.dt.uint32
U16 = mybir.dt.uint16
U8 = mybir.dt.uint8
FP8X4 = mybir.dt.float8_e4m3fn_x4
FP4X4 = mybir.dt.float4_e2m1fn_x4
COPY = mybir.ActivationFunctionType.Copy
MULT = mybir.AluOpType.mult
MAX = mybir.AluOpType.max

K, T, S, H, U, N = 512, 2048, 512, 512, 1024, 512
P = 128
PACK = 4
DECAY = 0.75
FLOPS = 2 * K * H * S + 2 * H * N * U
TILE_ORDER = (2, 0, 1, 3)
W1_VECTOR = 32
CHUNK = 128
N_CHUNKS = U // CHUNK
VECTOR_ROUNDS = ((0, 1), (1, 2), (2, 3))
SCALAR_ROUNDS = ((3, 5), (5, 8))
Z_QUANT = ((0, 1), (1, 2), (2, 3), (3, 5), (5, 7), (7, 8))
RESULT_STORES = ((1, 2), (2, 4), (4, 6), (6, 8))
OUT_QUANT = ((0, 1), (1, 2), (2, 4), (4, 6), (6, 7), (7, 8))
CODE_STORES = ((0, 4), (4, 7), (7, 8))


def load_scale_rows(queue, plane, rows):
    for q in range(4):
        queue.dma_start(out=plane[32 * q : 32 * q + 4, :].bitcast(I32), in_=rows[4 * q : 4 * q + 4, :].bitcast(I32))


def columns(run):
    return slice(run[0] * CHUNK, run[1] * CHUNK)


def ending_at(runs, c):
    return [run for run in runs if run[1] == c + 1]


def tile_picked_decaypage_none_po_kernel(tc, x_words, x_scales, w1, mem, w2_words, w2_scales, offs, slot, out_0, out_1, out_2):
    nc = tc.nc
    with ExitStack() as ctx:
        keep = ctx.enter_context(tc.tile_pool(name="keep", bufs=1))
        ring = ctx.enter_context(tc.tile_pool(name="ring", bufs=3))
        psum = ctx.enter_context(tc.psum_pool(name="psum", bufs=1))

        offs_sb = keep.tile([P, S // 16], U16)
        slot_sb = keep.tile([P, S // 16], U16)
        w1_raw = keep.tile([P, PACK, H], F32)
        x_table = keep.tile([P, T], U32)
        xs_table = keep.tile([P, T], U8)
        w2_raw = keep.tile([P, 2 * N], U8)
        w2s_raw = keep.tile([P, N], U8)
        mem_sb = [keep.tile([P, U], F32, name=f"mem{t}") for t in range(PACK)]
        mem_rows = mem.rearrange("(p t) w -> t p w", t=PACK)

        nc.vector.memset(xs_table[:].bitcast(I32), 0)
        nc.vector.memset(w2s_raw[:].bitcast(I32), 0)

        nc.sync.dma_start(out=offs_sb[:], in_=offs)
        nc.sync.dma_start(out=slot_sb[:], in_=slot)
        nc.sync.dma_start(out=w1_raw[:], in_=w1.rearrange("(p j) c -> p j c", j=PACK))
        load_scale_rows(nc.sync, xs_table, x_scales[0])
        nc.sync.dma_start(out=mem_sb[TILE_ORDER[0]][:], in_=mem_rows[TILE_ORDER[0]])
        nc.sync.dma_start(out=x_table[:].bitcast(I32), in_=x_words[0].rearrange("p n t -> p (n t)").bitcast(I32))
        for t in TILE_ORDER[1:]:
            nc.sync.dma_start(out=mem_sb[t][:], in_=mem_rows[t])
        nc.sync.dma_start(out=w2_raw[:].bitcast(I32), in_=w2_words[0].bitcast(I32))
        load_scale_rows(nc.sync, w2s_raw, w2_scales[0])

        w2_dealt = keep.tile([P, 2 * N], U8, align_bytes=64)
        w2s_dealt = keep.tile([P, N], U8, align_bytes=64)
        nc.gpsimd.tensor_copy(
            out=w2_dealt[:].rearrange("p (t m b) -> p t m b", t=PACK, b=2),
            in_=w2_raw[:].rearrange("p (m t b) -> p t m b", t=PACK, b=2),
        )

        w1_bf = keep.tile([P, PACK * H], BF16, align_bytes=64)
        w1_dst = w1_bf[:].rearrange("p (t m j) -> p m j t", t=PACK, j=PACK)
        w1_src = w1_raw[:].rearrange("p j (m t) -> p m j t", t=PACK)
        nc.vector.tensor_copy(out=w1_dst[:, :W1_VECTOR], in_=w1_src[:, :W1_VECTOR])
        nc.scalar.copy(out=w1_dst[:, W1_VECTOR:], in_=w1_src[:, W1_VECTOR:])

        xs_picked = keep.tile([P, S], U8, align_bytes=64)
        nc.vector.tensor_copy(out=xs_picked[:], in_=xs_table[:].indirect(offs_sb[:]))

        old = [keep.tile([P, S], F32, name=f"old{t}") for t in range(PACK)]

        def fetch_old(t):
            nc.vector.tensor_copy(out=old[t][:], in_=mem_sb[t][:].indirect(slot_sb[:]))

        fetch_old(TILE_ORDER[0])

        w1_codes = keep.tile([P, H], U32, align_bytes=64)
        w1_scales = keep.tile([P, H], U8, align_bytes=64)
        nc.vector.quantize_mx(out=w1_codes[:].bitcast(FP8X4), scales=w1_scales[:], in_=w1_bf[:])

        x_picked = keep.tile([P, S], U32, align_bytes=64)
        nc.vector.tensor_copy(out=x_picked[:], in_=x_table[:].indirect(offs_sb[:]))
        fetch_old(TILE_ORDER[1])

        z_bf = keep.tile([P, U, PACK], BF16, align_bytes=64)
        page = {}
        new = {}

        def decay(t):
            page[t] = ring.tile([P, U], F32, name="page")
            nc.scalar.activation(out=page[t][:], in_=mem_sb[t][:], func=COPY, scale=DECAY)

        def raise_old(t):
            y = psum.tile([P, S], F32, name="y", bufs=2)
            cols = slice(t * P, (t + 1) * P)
            nc.tensor.matmul_mx(
                out=y[:],
                lhsT=w1_codes[:, cols].bitcast(FP8X4),
                lhsT_scale=w1_scales[:, cols],
                rhs=x_picked[:].bitcast(FP8X4),
                rhs_scale=xs_picked[:],
                start=True,
                stop=True,
            )
            new[t] = ring.tile([P, S], F32, name="new")
            nc.vector.scalar_tensor_tensor(out=new[t][:], in0=old[t][:], scalar=DECAY, in1=y[:], op0=MULT, op1=MAX)

        for t in TILE_ORDER[:3]:
            decay(t)
        raise_old(TILE_ORDER[0])
        for i, t in enumerate(TILE_ORDER):
            if i + 1 < PACK:
                raise_old(TILE_ORDER[i + 1])
            if i + 2 < PACK:
                fetch_old(TILE_ORDER[i + 2])
            if i == PACK - 1:
                nc.gpsimd.tensor_copy(
                    out=w2s_dealt[:].rearrange("p (t m) -> p t m", t=PACK),
                    in_=w2s_raw[:].rearrange("p (m t) -> p t m", t=PACK),
                )
            nc.vector.tensor_copy(out=page[t][:].indirect(slot_sb[:]), in_=new[t][:])
            if i + 1 < PACK:
                nc.scalar.copy(out=z_bf[:, :, t], in_=page[t][:])
            if i == 0:
                decay(TILE_ORDER[3])
        last_t = TILE_ORDER[-1]

        z_codes = keep.tile([P, U], U32, align_bytes=64)
        z_scales = keep.tile([P, U], U8, align_bytes=64)
        res = keep.tile([P, PACK, U], F32)
        o_bf = keep.tile([P, U, PACK], BF16, align_bytes=64)
        o_codes = keep.tile([P, U], U32, align_bytes=64)
        o_scales = keep.tile([P, U // 4], U8, align_bytes=64)
        out_rows = out_0.rearrange("(p t) w -> p t w", t=PACK)
        code_rows = out_1[0].rearrange("p n t -> p (n t)").bitcast(I32)

        def quantize(codes, scales, values, cols):
            nc.vector.quantize_mx(
                out=codes[:, cols].bitcast(FP8X4),
                scales=scales,
                in_=values[:, cols, :].rearrange("p w t -> p (w t)"),
            )

        def second_product(c):
            cols = columns((c, c + 1))
            group = 2 if c == 0 else PACK
            for t0 in range(0, PACK, group):
                acc = psum.tile([P, group, CHUNK], F32, name="acc", bufs=6)
                for t in range(t0, t0 + group):
                    nc.tensor.matmul_mx(
                        out=acc[:, t - t0, :],
                        lhsT=w2_dealt[:, 2 * P * t : 2 * P * (t + 1)].bitcast(FP4X4),
                        lhsT_scale=w2s_dealt[:, P * t : P * (t + 1)],
                        rhs=z_codes[:, cols].bitcast(FP8X4),
                        rhs_scale=z_scales[:, cols],
                        start=True,
                        stop=True,
                    )
                nc.scalar.copy(out=res[:, t0 : t0 + group, cols], in_=acc[:])
                if c == 0:
                    nc.sync.dma_start(out=out_rows[:, t0 : t0 + group, cols], in_=res[:, t0 : t0 + group, cols])
            for run in ending_at(RESULT_STORES, c):
                nc.sync.dma_start(out=out_rows[:, :, columns(run)], in_=res[:, :, columns(run)])

        for run in SCALAR_ROUNDS:
            nc.scalar.copy(out=z_bf[:, columns(run), last_t], in_=page[last_t][:, columns(run)])
        nc.vector.tensor_copy(out=z_bf[:, columns(VECTOR_ROUNDS[0]), last_t], in_=page[last_t][:, columns(VECTOR_ROUNDS[0])])
        for i, run in enumerate(Z_QUANT):
            if i + 1 < len(VECTOR_ROUNDS):
                ahead = columns(VECTOR_ROUNDS[i + 1])
                nc.vector.tensor_copy(out=z_bf[:, ahead, last_t], in_=page[last_t][:, ahead])
            quantize(z_codes, z_scales[:, columns(run)], z_bf, columns(run))
            for c in range(run[0], run[1]):
                second_product(c)

        def round_result(run):
            dst = o_bf[:, columns(run), :].rearrange("p (c i) t -> p c t i", i=4)
            src = res[:, :, columns(run)].rearrange("p t (c i) -> p c t i", i=4)
            if run[1] == N_CHUNKS:
                nc.scalar.copy(out=dst, in_=src)
            else:
                nc.vector.tensor_copy(out=dst, in_=src)

        round_result(OUT_QUANT[0])
        for i, run in enumerate(OUT_QUANT):
            if i + 1 < len(OUT_QUANT):
                round_result(OUT_QUANT[i + 1])
            quarter = run[0] // 2
            local = columns((run[0] - 2 * quarter, run[1] - 2 * quarter))
            quantize(o_codes, o_scales[4 * quarter :, local], o_bf, columns(run))
            for stored in ending_at(CODE_STORES, run[1] - 1):
                nc.sync.dma_start(out=code_rows[:, columns(stored)], in_=o_codes[:, columns(stored)].bitcast(I32))
        for q in range(4):
            queue = nc.sync if q % 2 == 0 else nc.scalar
            queue.dma_start(out=out_2[0, 4 * q : 4 * q + 4, :].bitcast(I32).rearrange("r (j c) -> j r c", j=4), in_=o_scales[32 * q : 32 * q + 16, :].bitcast(I32))
